import numpy as np
import ml_dtypes


def mxq(x, axis, fmt="e4m3"):
    dtype, down = {"e4m3": (ml_dtypes.float8_e4m3fn, 7), "e5m2": (ml_dtypes.float8_e5m2, 14)}[fmt]
    v = np.moveaxis(np.asarray(x, np.float32).astype(ml_dtypes.bfloat16).astype(np.float64), axis, -1)
    blocks = v.reshape(v.shape[:-1] + (-1, 32))
    amax = np.abs(blocks).max(-1, keepdims=True)
    byte = np.maximum(np.where(amax > 0, np.frexp(amax)[1] - 1 + 127, 0) - down, 1)
    scale = np.exp2(byte - 127.0)
    codes = (blocks / scale).astype(np.float32).astype(dtype).astype(np.float64)
    return np.moveaxis((codes * scale).reshape(v.shape), -1, axis)


WIDE = False


def mx_kscale(k):
    if not WIDE:
        return np.ones(k)
    levels = np.array([10, -10, 5, -5, 0])
    if k % 512:
        return np.exp2(np.random.permutation(np.resize(levels, k // 32))).repeat(32)
    a = np.empty((k // 512, 16))
    for p in range(k // 512):
        a[p, :8] = np.random.permutation(np.resize(levels, 8))
        for g in range(8):
            far = levels[np.abs(levels - a[p, g]) >= 10]
            a[p, g + 8] = far[np.random.randint(len(far))]
    return np.exp2(a.ravel()).repeat(32)


def f64(x):
    return np.asarray(x).astype(np.float64)


def striped8(idx):
    return np.asarray(idx).reshape(8, -1, 16).transpose(0, 2, 1).reshape(128, -1).astype(np.uint16)


def unstriped8(offs):
    return offs.reshape(8, 16, -1).transpose(0, 2, 1).reshape(8, -1).astype(np.int64)


def pick8(x, idx, run):
    r = np.arange(len(x))
    return x[r[:, None], idx[r % (8 * run) // run]]


E2M1 = np.array([0.0, 0.5, 1.0, 1.5, 2.0, 3.0, 4.0, 6.0, -0.0, -0.5, -1.0, -1.5, -2.0, -3.0, -4.0, -6.0])


def pack_weight(w, fmt):
    k, n = w.shape
    w = f64(np.asarray(w, np.float32).astype(ml_dtypes.bfloat16)).reshape(k // 32, 32, n)
    amax = np.abs(w).max(1)
    if fmt == "e4m3":
        byte = np.frexp(amax)[1] - 1 + 127 - 7
    else:
        mant, ex = np.frexp(amax / 6.0)
        byte = np.where(mant > 0.5, ex, ex - 1) + 127
    byte = np.clip(np.where(amax > 0, byte, 1), 1, 254)
    scaled = (w * np.exp2(127.0 - byte)[:, None, :]).reshape(k, n).astype(np.float32)
    by_word = np.ascontiguousarray(scaled.reshape(k // 512, 128, 4, n).transpose(0, 1, 3, 2))
    if fmt == "e4m3":
        words = by_word.astype(ml_dtypes.float8_e4m3fn).view(np.uint8)
    else:
        c = by_word.astype(ml_dtypes.float4_e2m1fn).view(np.uint8) & 0xF
        words = (c[..., 0::2] | (c[..., 1::2] << 4)).reshape(k // 512, 128, 2 * n)
    return np.ascontiguousarray(words), np.ascontiguousarray(byte.astype(np.uint8).reshape(k // 512, 16, n))


def unpack_weight(words, scales, fmt):
    g, _, n = scales.shape
    words = np.ascontiguousarray(words).reshape(g, 128, n, -1)
    if fmt == "e4m3":
        vals = words.view(ml_dtypes.float8_e4m3fn).astype(np.float64)
    else:
        nib = np.empty((g, 128, n, 4), np.uint8)
        nib[..., 0::2] = words & 0xF
        nib[..., 1::2] = words >> 4
        vals = E2M1[nib]
    vals = vals * np.repeat(np.exp2(scales.astype(np.float64) - 127.0), 8, axis=1)[..., None]
    return vals.transpose(0, 1, 3, 2).reshape(g * 512, n)


D, T, I, Q = 512, 1024, 512, 128


def setup_inputs():
    n = np.random.standard_normal
    idx = np.stack([np.random.permutation(T)[:I] for _ in range(8)])
    idx2 = np.stack([np.random.permutation(T)[:I] for _ in range(8)])
    idx3 = np.stack([np.random.permutation(T)[:I] for _ in range(8)])
    fd = mx_kscale(D)
    keysp = pack_weight(n((D, T)) / fd[:, None], "e2m1")
    return {
        "query": (n((D, Q)) * 0.9 / np.sqrt(D) * fd[:, None]).astype(np.float32),
        "keys_words": keysp[0],
        "keys_scales": keysp[1],
        "lam": (np.random.uniform(0.3, 0.9, (Q, 1))).astype(np.float32),
        "bar": (np.random.uniform(0.0, 0.8, (Q, 1))).astype(np.float32),
        "reserve": (np.random.uniform(20.0, 80.0, (Q, 1))).astype(np.float32),
        "old": (np.random.uniform(0.0, 2.0, (Q, T))).astype(np.float32),
        "fade": (np.random.uniform(0.3, 0.9, (Q, 1))).astype(np.float32),
        "offs": striped8(idx),
        "offs2": striped8(idx2),
        "offs3": striped8(idx3),
    }


def reference(query, keys_words, keys_scales, lam, bar, reserve, old, fade, offs, offs2, offs3):
    idx = unstriped8(offs)
    idx2 = unstriped8(offs2)
    idx3 = unstriped8(offs3)
    keysu = unpack_weight(keys_words, keys_scales, "e2m1")
    queryq = mxq(f64(query), 0, "e4m3")
    a = queryq.T @ keysu
    s = pick8(a, idx, 16) + np.maximum(pick8(a, idx2, 16), pick8(a, idx3, 16)) * f64(lam)
    ce = s - np.mean(s, axis=1, keepdims=True)
    sd = np.sqrt(np.mean(np.square(ce), axis=1, keepdims=True) + 0.1)
    p = np.square(np.maximum(ce / sd - f64(bar), 0.0))
    w = p / (np.sum(p, axis=1, keepdims=True) + f64(reserve))
    ws = w * 256.0
    wf = np.zeros((Q, T))
    wf[np.arange(Q)[:, None], idx[np.arange(Q) % 128 // 16]] = ws
    y = f64(old) * f64(fade) + wf
    return y

@@ -1,0 +1,168 @@
+from contextlib import ExitStack
+
+import concourse.mybir as mybir
+
+D, T, SLOTS, Q = 512, 1024, 512, 128
+FLOPS = 2 * D * T * Q
+
+F32 = mybir.dt.float32
+BF16 = mybir.dt.bfloat16
+I32 = mybir.dt.int32
+U32 = mybir.dt.uint32
+U16 = mybir.dt.uint16
+U8 = mybir.dt.uint8
+FP8X4 = mybir.dt.float8_e4m3fn_x4
+FP4X4 = mybir.dt.float4_e2m1fn_x4
+ALU = mybir.AluOpType
+ACT = mybir.ActivationFunctionType
+
+P = 128
+PACK = 4
+PER_COLUMN = 16
+HALF = SLOTS // 2
+MM_WIDTHS = (256, 256, 256, 128, 128)
+V_SHARE = 288
+STORE_PIECE = 256
+
+
+def tile_attend_lookahead_outliers_counts_heads_kernel(
+    tc, query, keys_words, keys_scales, lam, bar, reserve, old, fade, offs, offs2, offs3, out
+):
+    nc = tc.nc
+    with ExitStack() as ctx:
+        sb = ctx.enter_context(tc.tile_pool(name="sb", bufs=1))
+        ps = ctx.enter_context(tc.psum_pool(name="ps", bufs=1))
+
+        key_scales = sb.tile([P, T], U8, align_bytes=64)
+        nc.gpsimd.memset(key_scales[:].bitcast(I32), 0)
+
+        q_raw = sb.tile([P, PACK, Q], F32)
+        nc.sync.dma_start(out=q_raw[:], in_=query.rearrange("(p j) q -> p j q", j=PACK))
+        key_words = sb.tile([P, 2 * T], U8, align_bytes=64)
+        nc.sync.dma_start(out=key_words[:].bitcast(I32), in_=keys_words[0].bitcast(I32))
+        for quad in range(4):
+            nc.sync.dma_start(
+                out=key_scales[32 * quad : 32 * quad + 4, :].bitcast(I32),
+                in_=keys_scales[0, 4 * quad : 4 * quad + 4, :].bitcast(I32),
+            )
+        list3 = sb.tile([P, SLOTS // PER_COLUMN], U16)
+        nc.sync.dma_start(list3[:], offs3)
+        list2 = sb.tile([P, SLOTS // PER_COLUMN], U16)
+        nc.sync.dma_start(list2[:], offs2)
+        list1 = sb.tile([P, SLOTS // PER_COLUMN], U16)
+        nc.sync.dma_start(list1[:], offs)
+
+        lam_sb = sb.tile([P, 1], F32)
+        nc.sync.dma_start(out=lam_sb[:], in_=lam)
+        bar_sb = sb.tile([P, 1], F32)
+        nc.sync.dma_start(out=bar_sb[:], in_=bar)
+        reserve_sb = sb.tile([P, 1], F32)
+        nc.sync.dma_start(out=reserve_sb[:], in_=reserve)
+        fade_sb = sb.tile([P, 1], F32)
+        nc.sync.dma_start(out=fade_sb[:], in_=fade)
+
+        old_sb = sb.tile([P, T], F32)
+        nc.sync.dma_start(out=old_sb[:], in_=old)
+        neg_bar = sb.tile([P, 1], F32)
+        nc.vector.tensor_scalar(neg_bar[:], bar_sb[:], -1.0, None, ALU.mult)
+
+        placed = sb.tile([P, T], F32)
+        nc.vector.memset(placed[:], 0.0)
+
+        q_bf = sb.tile([P, Q, PACK], BF16, align_bytes=64)
+        q_codes = sb.tile([P, Q], U32, align_bytes=64)
+        q_scales = sb.tile([P, Q], U8, align_bytes=64)
+        for q0 in range(0, Q, Q // 2):
+            cols = slice(q0, q0 + Q // 2)
+            nc.vector.tensor_copy(
+                out=q_bf[:, cols, :].rearrange("p (c i) j -> p c j i", i=4),
+                in_=q_raw[:, :, cols].rearrange("p j (c i) -> p c j i", i=4),
+            )
+        for q0 in range(0, Q, Q // 2):
+            cols = slice(q0, q0 + Q // 2)
+            nc.vector.quantize_mx(
+                out=q_codes[:, cols].bitcast(FP8X4),
+                scales=q_scales[:, cols],
+                in_=q_bf[:, cols, :].rearrange("p q j -> p (q j)"),
+            )
+
+        scores = sb.tile([P, T], F32)
+        t0 = 0
+        for n, width in enumerate(MM_WIDTHS):
+            bank = ps.tile([P, 512], F32, name="bank%d" % n)
+            nc.tensor.matmul_mx(
+                out=bank[:, 0:width],
+                lhsT=q_codes[:].bitcast(FP8X4),
+                lhsT_scale=q_scales[:],
+                rhs=key_words[:, 2 * t0 : 2 * (t0 + width)].bitcast(FP4X4),
+                rhs_scale=key_scales[:, t0 : t0 + width],
+                start=True,
+                stop=True,
+            )
+            if n % 2 == 1:
+                nc.scalar.copy(out=scores[:, t0 : t0 + width], in_=bank[:, 0:width])
+            else:
+                nc.vector.tensor_copy(out=scores[:, t0 : t0 + width], in_=bank[:, 0:width])
+            t0 += width
+
+        def looked_up(lst, h):
+            cols = HALF // PER_COLUMN
+            return scores[:].indirect(lst[:, h * cols : (h + 1) * cols])
+
+        g1 = [sb.tile([P, HALF], F32, name="g1_%d" % h) for h in range(2)]
+        g2 = [sb.tile([P, HALF], F32, name="g2_%d" % h) for h in range(2)]
+        g3 = [sb.tile([P, HALF], F32, name="g3_%d" % h) for h in range(2)]
+        larger = [sb.tile([P, HALF], F32, name="larger_%d" % h) for h in range(2)]
+        s = sb.tile([P, SLOTS], F32)
+        stats = sb.tile([P, 3, 6], F32)
+
+        nc.scalar.activation(g3[0][:], looked_up(list3, 0), ACT.Copy)
+        nc.vector.tensor_copy(g2[0][:], looked_up(list2, 0))
+        nc.scalar.activation(g2[1][:], looked_up(list2, 1), ACT.Copy)
+        nc.vector.tensor_copy(g1[0][:], looked_up(list1, 0))
+        nc.scalar.activation(g3[1][:], looked_up(list3, 1), ACT.Copy)
+        nc.scalar.activation(g1[1][:], looked_up(list1, 1), ACT.Copy)
+        for h in range(2):
+            nc.vector.tensor_tensor(larger[h][:], g2[h][:], g3[h][:], ALU.max)
+        runs = [(0, 0, HALF), (1, 0, HALF // 2), (1, HALF // 2, HALF)]
+        for n, (h, lo, hi) in enumerate(runs):
+            cols = slice(h * HALF + lo, h * HALF + hi)
+            nc.vector.scalar_tensor_tensor(
+                s[:, cols], larger[h][:, lo:hi], lam_sb[:], g1[h][:, lo:hi], ALU.mult, ALU.add
+            )
+        for n, (h, lo, hi) in enumerate(runs):
+            nc.vector.bn_stats(stats[:, n, :], s[:, h * HALF + lo : h * HALF + hi])
+        mean_var = sb.tile([P, 2], F32)
+        nc.vector.bn_aggr(mean_var[:], stats[:].rearrange("p h k -> p (h k)"))
+
+        inv_sd = sb.tile([P, 1], F32)
+        nc.scalar.activation(inv_sd[:], mean_var[:, 1:2], ACT.Abs_reciprocal_sqrt, bias=0.1)
+        centred = sb.tile([P, SLOTS], F32)
+        nc.vector.tensor_scalar(centred[:], s[:], mean_var[:, 0:1], None, ALU.subtract)
+        part = sb.tile([P, SLOTS], F32)
+        excess = sb.tile([P, V_SHARE], F32)
+        nc.vector.tensor_scalar(excess[:], centred[:, 0:V_SHARE], inv_sd[:], bar_sb[:], ALU.mult, ALU.subtract)
+        sum_v = sb.tile([P, 1], F32)
+        nc.vector.scalar_tensor_tensor(
+            part[:, 0:V_SHARE], excess[:], 0.0, excess[:], ALU.max, ALU.mult, accum_out=sum_v[:]
+        )
+        above = sb.tile([P, SLOTS - V_SHARE], F32)
+        nc.scalar.activation(above[:], centred[:, V_SHARE:SLOTS], ACT.Relu, bias=neg_bar[:], scale=inv_sd[:])
+        sum_s = sb.tile([P, 1], F32)
+        nc.scalar.activation(part[:, V_SHARE:SLOTS], above[:], ACT.Square, accum_out=sum_s[:])
+        divisor = sb.tile([P, 1], F32)
+        nc.vector.tensor_scalar(divisor[:], sum_v[:], sum_s[:], reserve_sb[:], ALU.add, ALU.add)
+        factor = sb.tile([P, 1], F32)
+        nc.vector.reciprocal(factor[:], divisor[:])
+        ws = sb.tile([P, SLOTS], F32)
+        nc.vector.tensor_scalar(ws[:], part[:], factor[:], 256.0, ALU.mult, ALU.mult)
+        nc.vector.tensor_copy(placed[:].indirect(list1[:]), ws[:])
+
+        for n, t0 in enumerate(range(0, T, STORE_PIECE)):
+            cols = slice(t0, t0 + STORE_PIECE)
+            result = sb.tile([P, STORE_PIECE], F32, name="result_%d" % n)
+            nc.vector.scalar_tensor_tensor(
+                result[:], old_sb[:, cols], fade_sb[:], placed[:, cols], ALU.mult, ALU.add
+            )
+            queue = nc.sync if n % 2 == 0 else nc.scalar
+            queue.dma_start(out=out[:, cols], in_=result[:])

@@ -34,7 +34,7 @@ def tile_attend_lookahead_outliers_counts_heads_kernel(
         ps = ctx.enter_context(tc.psum_pool(name="ps", bufs=1))
 
         key_scales = sb.tile([P, T], U8, align_bytes=64)
-        nc.gpsimd.memset(key_scales[:].bitcast(I32), 0)
+        nc.vector.memset(key_scales[:].bitcast(I32), 0)
 
         q_raw = sb.tile([P, PACK, Q], F32)
         nc.sync.dma_start(out=q_raw[:], in_=query.rearrange("(p j) q -> p j q", j=PACK))
@@ -64,7 +64,7 @@ def tile_attend_lookahead_outliers_counts_heads_kernel(
         old_sb = sb.tile([P, T], F32)
         nc.sync.dma_start(out=old_sb[:], in_=old)
         neg_bar = sb.tile([P, 1], F32)
-        nc.vector.tensor_scalar(neg_bar[:], bar_sb[:], -1.0, None, ALU.mult)
+        nc.gpsimd.tensor_scalar(neg_bar[:], bar_sb[:], -1.0, 0.0, ALU.mult, ALU.add)
 
         placed = sb.tile([P, T], F32)
         nc.vector.memset(placed[:], 0.0)
@@ -122,23 +122,28 @@ def tile_attend_lookahead_outliers_counts_heads_kernel(
         nc.vector.tensor_copy(g1[0][:], looked_up(list1, 0))
         nc.scalar.activation(g3[1][:], looked_up(list3, 1), ACT.Copy)
         nc.scalar.activation(g1[1][:], looked_up(list1, 1), ACT.Copy)
-        for h in range(2):
-            nc.vector.tensor_tensor(larger[h][:], g2[h][:], g3[h][:], ALU.max)
-        runs = [(0, 0, HALF), (1, 0, HALF // 2), (1, HALF // 2, HALF)]
-        for n, (h, lo, hi) in enumerate(runs):
-            cols = slice(h * HALF + lo, h * HALF + hi)
+        def slot_scores(h, lo, hi):
             nc.vector.scalar_tensor_tensor(
-                s[:, cols], larger[h][:, lo:hi], lam_sb[:], g1[h][:, lo:hi], ALU.mult, ALU.add
+                s[:, h * HALF + lo : h * HALF + hi], larger[h][:, lo:hi], lam_sb[:], g1[h][:, lo:hi], ALU.mult, ALU.add
             )
-        for n, (h, lo, hi) in enumerate(runs):
-            nc.vector.bn_stats(stats[:, n, :], s[:, h * HALF + lo : h * HALF + hi])
+
+        nc.vector.tensor_tensor(larger[0][:], g2[0][:], g3[0][:], ALU.max)
+        slot_scores(0, 0, HALF)
+        nc.vector.tensor_tensor(larger[1][:], g2[1][:], g3[1][:], ALU.max)
+        nc.vector.bn_stats(stats[:, 0, :], s[:, 0:HALF])
+        quarters = [(0, HALF // 2), (HALF // 2, HALF)]
+        for lo, hi in quarters:
+            slot_scores(1, lo, hi)
+        for n, (lo, hi) in enumerate(quarters):
+            nc.vector.bn_stats(stats[:, 1 + n, :], s[:, HALF + lo : HALF + hi])
         mean_var = sb.tile([P, 2], F32)
         nc.vector.bn_aggr(mean_var[:], stats[:].rearrange("p h k -> p (h k)"))
 
         inv_sd = sb.tile([P, 1], F32)
         nc.scalar.activation(inv_sd[:], mean_var[:, 1:2], ACT.Abs_reciprocal_sqrt, bias=0.1)
         centred = sb.tile([P, SLOTS], F32)
-        nc.vector.tensor_scalar(centred[:], s[:], mean_var[:, 0:1], None, ALU.subtract)
+        for cols in (slice(V_SHARE, SLOTS), slice(0, V_SHARE)):
+            nc.vector.tensor_scalar(centred[:, cols], s[:, cols], mean_var[:, 0:1], None, ALU.subtract)
         part = sb.tile([P, SLOTS], F32)
         excess = sb.tile([P, V_SHARE], F32)
         nc.vector.tensor_scalar(excess[:], centred[:, 0:V_SHARE], inv_sd[:], bar_sb[:], ALU.mult, ALU.subtract)

@@ -53,9 +53,9 @@ def tile_attend_lookahead_outliers_counts_heads_kernel(
         nc.sync.dma_start(list1[:], offs)
 
         lam_sb = sb.tile([P, 1], F32)
-        nc.sync.dma_start(out=lam_sb[:], in_=lam)
+        nc.gpsimd.dma_start(out=lam_sb[:], in_=lam)
         bar_sb = sb.tile([P, 1], F32)
-        nc.sync.dma_start(out=bar_sb[:], in_=bar)
+        nc.gpsimd.dma_start(out=bar_sb[:], in_=bar)
         reserve_sb = sb.tile([P, 1], F32)
         nc.sync.dma_start(out=reserve_sb[:], in_=reserve)
         fade_sb = sb.tile([P, 1], F32)

from contextlib import ExitStack

import concourse.mybir as mybir

D, T, SLOTS, Q = 512, 1024, 512, 128
FLOPS = 2 * D * T * Q

F32 = mybir.dt.float32
BF16 = mybir.dt.bfloat16
I32 = mybir.dt.int32
U32 = mybir.dt.uint32
U16 = mybir.dt.uint16
U8 = mybir.dt.uint8
FP8X4 = mybir.dt.float8_e4m3fn_x4
FP4X4 = mybir.dt.float4_e2m1fn_x4
ALU = mybir.AluOpType
ACT = mybir.ActivationFunctionType

P = 128
PACK = 4
PER_COLUMN = 16
HALF = SLOTS // 2
MM_WIDTHS = (256, 256, 256, 128, 128)
V_SHARE = 288
STORE_PIECE = 256


def tile_attend_lookahead_outliers_counts_heads_kernel(
    tc, query, keys_words, keys_scales, lam, bar, reserve, old, fade, offs, offs2, offs3, out
):
    nc = tc.nc
    with ExitStack() as ctx:
        sb = ctx.enter_context(tc.tile_pool(name="sb", bufs=1))
        ps = ctx.enter_context(tc.psum_pool(name="ps", bufs=1))

        key_scales = sb.tile([P, T], U8, align_bytes=64)
        nc.vector.memset(key_scales[:].bitcast(I32), 0)

        q_raw = sb.tile([P, PACK, Q], F32)
        nc.sync.dma_start(out=q_raw[:], in_=query.rearrange("(p j) q -> p j q", j=PACK))
        key_words = sb.tile([P, 2 * T], U8, align_bytes=64)
        nc.sync.dma_start(out=key_words[:].bitcast(I32), in_=keys_words[0].bitcast(I32))
        for quad in range(4):
            nc.sync.dma_start(
                out=key_scales[32 * quad : 32 * quad + 4, :].bitcast(I32),
                in_=keys_scales[0, 4 * quad : 4 * quad + 4, :].bitcast(I32),
            )
        list3 = sb.tile([P, SLOTS // PER_COLUMN], U16)
        nc.sync.dma_start(list3[:], offs3)
        list2 = sb.tile([P, SLOTS // PER_COLUMN], U16)
        nc.sync.dma_start(list2[:], offs2)
        list1 = sb.tile([P, SLOTS // PER_COLUMN], U16)
        nc.sync.dma_start(list1[:], offs)

        lam_sb = sb.tile([P, 1], F32)
        nc.gpsimd.dma_start(out=lam_sb[:], in_=lam)
        bar_sb = sb.tile([P, 1], F32)
        nc.gpsimd.dma_start(out=bar_sb[:], in_=bar)
        reserve_sb = sb.tile([P, 1], F32)
        nc.sync.dma_start(out=reserve_sb[:], in_=reserve)
        fade_sb = sb.tile([P, 1], F32)
        nc.sync.dma_start(out=fade_sb[:], in_=fade)

        old_sb = sb.tile([P, T], F32)
        nc.sync.dma_start(out=old_sb[:], in_=old)
        neg_bar = sb.tile([P, 1], F32)
        nc.gpsimd.tensor_scalar(neg_bar[:], bar_sb[:], -1.0, 0.0, ALU.mult, ALU.add)

        placed = sb.tile([P, T], F32)
        nc.vector.memset(placed[:], 0.0)

        q_bf = sb.tile([P, Q, PACK], BF16, align_bytes=64)
        q_codes = sb.tile([P, Q], U32, align_bytes=64)
        q_scales = sb.tile([P, Q], U8, align_bytes=64)
        for q0 in range(0, Q, Q // 2):
            cols = slice(q0, q0 + Q // 2)
            nc.vector.tensor_copy(
                out=q_bf[:, cols, :].rearrange("p (c i) j -> p c j i", i=4),
                in_=q_raw[:, :, cols].rearrange("p j (c i) -> p c j i", i=4),
            )
        for q0 in range(0, Q, Q // 2):
            cols = slice(q0, q0 + Q // 2)
            nc.vector.quantize_mx(
                out=q_codes[:, cols].bitcast(FP8X4),
                scales=q_scales[:, cols],
                in_=q_bf[:, cols, :].rearrange("p q j -> p (q j)"),
            )

        scores = sb.tile([P, T], F32)
        t0 = 0
        for n, width in enumerate(MM_WIDTHS):
            bank = ps.tile([P, 512], F32, name="bank%d" % n)
            nc.tensor.matmul_mx(
                out=bank[:, 0:width],
                lhsT=q_codes[:].bitcast(FP8X4),
                lhsT_scale=q_scales[:],
                rhs=key_words[:, 2 * t0 : 2 * (t0 + width)].bitcast(FP4X4),
                rhs_scale=key_scales[:, t0 : t0 + width],
                start=True,
                stop=True,
            )
            if n % 2 == 1:
                nc.scalar.copy(out=scores[:, t0 : t0 + width], in_=bank[:, 0:width])
            else:
                nc.vector.tensor_copy(out=scores[:, t0 : t0 + width], in_=bank[:, 0:width])
            t0 += width

        def looked_up(lst, h):
            cols = HALF // PER_COLUMN
            return scores[:].indirect(lst[:, h * cols : (h + 1) * cols])

        g1 = [sb.tile([P, HALF], F32, name="g1_%d" % h) for h in range(2)]
        g2 = [sb.tile([P, HALF], F32, name="g2_%d" % h) for h in range(2)]
        g3 = [sb.tile([P, HALF], F32, name="g3_%d" % h) for h in range(2)]
        larger = [sb.tile([P, HALF], F32, name="larger_%d" % h) for h in range(2)]
        s = sb.tile([P, SLOTS], F32)
        stats = sb.tile([P, 3, 6], F32)

        nc.scalar.activation(g3[0][:], looked_up(list3, 0), ACT.Copy)
        nc.vector.tensor_copy(g2[0][:], looked_up(list2, 0))
        nc.scalar.activation(g2[1][:], looked_up(list2, 1), ACT.Copy)
        nc.vector.tensor_copy(g1[0][:], looked_up(list1, 0))
        nc.scalar.activation(g3[1][:], looked_up(list3, 1), ACT.Copy)
        nc.scalar.activation(g1[1][:], looked_up(list1, 1), ACT.Copy)
        def slot_scores(h, lo, hi):
            nc.vector.scalar_tensor_tensor(
                s[:, h * HALF + lo : h * HALF + hi], larger[h][:, lo:hi], lam_sb[:], g1[h][:, lo:hi], ALU.mult, ALU.add
            )

        nc.vector.tensor_tensor(larger[0][:], g2[0][:], g3[0][:], ALU.max)
        slot_scores(0, 0, HALF)
        nc.vector.tensor_tensor(larger[1][:], g2[1][:], g3[1][:], ALU.max)
        nc.vector.bn_stats(stats[:, 0, :], s[:, 0:HALF])
        quarters = [(0, HALF // 2), (HALF // 2, HALF)]
        for lo, hi in quarters:
            slot_scores(1, lo, hi)
        for n, (lo, hi) in enumerate(quarters):
            nc.vector.bn_stats(stats[:, 1 + n, :], s[:, HALF + lo : HALF + hi])
        mean_var = sb.tile([P, 2], F32)
        nc.vector.bn_aggr(mean_var[:], stats[:].rearrange("p h k -> p (h k)"))

        inv_sd = sb.tile([P, 1], F32)
        nc.scalar.activation(inv_sd[:], mean_var[:, 1:2], ACT.Abs_reciprocal_sqrt, bias=0.1)
        centred = sb.tile([P, SLOTS], F32)
        for cols in (slice(V_SHARE, SLOTS), slice(0, V_SHARE)):
            nc.vector.tensor_scalar(centred[:, cols], s[:, cols], mean_var[:, 0:1], None, ALU.subtract)
        part = sb.tile([P, SLOTS], F32)
        excess = sb.tile([P, V_SHARE], F32)
        nc.vector.tensor_scalar(excess[:], centred[:, 0:V_SHARE], inv_sd[:], bar_sb[:], ALU.mult, ALU.subtract)
        sum_v = sb.tile([P, 1], F32)
        nc.vector.scalar_tensor_tensor(
            part[:, 0:V_SHARE], excess[:], 0.0, excess[:], ALU.max, ALU.mult, accum_out=sum_v[:]
        )
        above = sb.tile([P, SLOTS - V_SHARE], F32)
        nc.scalar.activation(above[:], centred[:, V_SHARE:SLOTS], ACT.Relu, bias=neg_bar[:], scale=inv_sd[:])
        sum_s = sb.tile([P, 1], F32)
        nc.scalar.activation(part[:, V_SHARE:SLOTS], above[:], ACT.Square, accum_out=sum_s[:])
        divisor = sb.tile([P, 1], F32)
        nc.vector.tensor_scalar(divisor[:], sum_v[:], sum_s[:], reserve_sb[:], ALU.add, ALU.add)
        factor = sb.tile([P, 1], F32)
        nc.vector.reciprocal(factor[:], divisor[:])
        ws = sb.tile([P, SLOTS], F32)
        nc.vector.tensor_scalar(ws[:], part[:], factor[:], 256.0, ALU.mult, ALU.mult)
        nc.vector.tensor_copy(placed[:].indirect(list1[:]), ws[:])

        for n, t0 in enumerate(range(0, T, STORE_PIECE)):
            cols = slice(t0, t0 + STORE_PIECE)
            result = sb.tile([P, STORE_PIECE], F32, name="result_%d" % n)
            nc.vector.scalar_tensor_tensor(
                result[:], old_sb[:, cols], fade_sb[:], placed[:, cols], ALU.mult, ALU.add
            )
            queue = nc.sync if n % 2 == 0 else nc.scalar
            queue.dma_start(out=out[:, cols], in_=result[:])
